import numpy as np
import ml_dtypes


def mxq(x, axis, fmt="e4m3"):
    dtype, down = {"e4m3": (ml_dtypes.float8_e4m3fn, 7), "e5m2": (ml_dtypes.float8_e5m2, 14)}[fmt]
    v = np.moveaxis(np.asarray(x, np.float32).astype(ml_dtypes.bfloat16).astype(np.float64), axis, -1)
    blocks = v.reshape(v.shape[:-1] + (-1, 32))
    amax = np.abs(blocks).max(-1, keepdims=True)
    byte = np.maximum(np.where(amax > 0, np.frexp(amax)[1] - 1 + 127, 0) - down, 1)
    scale = np.exp2(byte - 127.0)
    codes = (blocks / scale).astype(np.float32).astype(dtype).astype(np.float64)
    return np.moveaxis((codes * scale).reshape(v.shape), -1, axis)


WIDE = False


def mx_kscale(k):
    if not WIDE:
        return np.ones(k)
    levels = np.array([10, -10, 5, -5, 0])
    if k % 512:
        return np.exp2(np.random.permutation(np.resize(levels, k // 32))).repeat(32)
    a = np.empty((k // 512, 16))
    for p in range(k // 512):
        a[p, :8] = np.random.permutation(np.resize(levels, 8))
        for g in range(8):
            far = levels[np.abs(levels - a[p, g]) >= 10]
            a[p, g + 8] = far[np.random.randint(len(far))]
    return np.exp2(a.ravel()).repeat(32)


def f64(x):
    return np.asarray(x).astype(np.float64)


def striped(idx):
    return np.tile(idx.reshape(-1, 16).T, (8, 1)).astype(np.uint16)


def unstriped(offs):
    return offs[:16].T.reshape(-1).astype(np.int64)


E2M1 = np.array([0.0, 0.5, 1.0, 1.5, 2.0, 3.0, 4.0, 6.0, -0.0, -0.5, -1.0, -1.5, -2.0, -3.0, -4.0, -6.0])


def pack_weight(w, fmt):
    k, n = w.shape
    w = f64(np.asarray(w, np.float32).astype(ml_dtypes.bfloat16)).reshape(k // 32, 32, n)
    amax = np.abs(w).max(1)
    if fmt == "e4m3":
        byte = np.frexp(amax)[1] - 1 + 127 - 7
    else:
        mant, ex = np.frexp(amax / 6.0)
        byte = np.where(mant > 0.5, ex, ex - 1) + 127
    byte = np.clip(np.where(amax > 0, byte, 1), 1, 254)
    scaled = (w * np.exp2(127.0 - byte)[:, None, :]).reshape(k, n).astype(np.float32)
    by_word = np.ascontiguousarray(scaled.reshape(k // 512, 128, 4, n).transpose(0, 1, 3, 2))
    if fmt == "e4m3":
        words = by_word.astype(ml_dtypes.float8_e4m3fn).view(np.uint8)
    else:
        c = by_word.astype(ml_dtypes.float4_e2m1fn).view(np.uint8) & 0xF
        words = (c[..., 0::2] | (c[..., 1::2] << 4)).reshape(k // 512, 128, 2 * n)
    return np.ascontiguousarray(words), np.ascontiguousarray(byte.astype(np.uint8).reshape(k // 512, 16, n))


def unpack_weight(words, scales, fmt):
    g, _, n = scales.shape
    words = np.ascontiguousarray(words).reshape(g, 128, n, -1)
    if fmt == "e4m3":
        vals = words.view(ml_dtypes.float8_e4m3fn).astype(np.float64)
    else:
        nib = np.empty((g, 128, n, 4), np.uint8)
        nib[..., 0::2] = words & 0xF
        nib[..., 1::2] = words >> 4
        vals = E2M1[nib]
    vals = vals * np.repeat(np.exp2(scales.astype(np.float64) - 127.0), 8, axis=1)[..., None]
    return vals.transpose(0, 1, 3, 2).reshape(g * 512, n)


def gelu(v):
    return 0.5 * v * (1.0 + np.tanh(np.sqrt(2.0 / np.pi) * (v + 0.044715 * v**3)))


K, H, T, S, S2, T3, T2, P = 1024, 1024, 2048, 512, 1024, 2048, 1024, 512

def setup_inputs():
    n = np.random.standard_normal
    s = mx_kscale(K)[:, None]
    u = mx_kscale(H)[:, None]
    tab_words, tab_scales = pack_weight(n((K, T)) * s, "e4m3")
    tab2_words, tab2_scales = pack_weight(n((H, T3)) / np.sqrt(H) / u, "e4m3")
    w2_words, w2_scales = pack_weight(n((K, H)) / np.sqrt(K) / s * u.T, "e2m1")
    return {
        "tab_words": tab_words, "tab_scales": tab_scales,
        "tab2_words": tab2_words, "tab2_scales": tab2_scales,
        "w1": (0.55 * n((K, H)) / np.sqrt(K) / s).astype(np.float32),
        "w2_words": w2_words, "w2_scales": w2_scales,
        "res": (0.7 * n((H, S)) * u).astype(np.float32),
        "wgs": np.exp(0.3 * n((128, S))).astype(np.float32),
        "page0": (n((H, T2)) * u).astype(np.float32),
        "wl": np.exp(0.4 * n(S2)).astype(np.float32),
        "offs": striped(np.random.permutation(T)[:S]),
        "offs2": striped(np.random.permutation(T3)[:S2]),
        "offs3": striped(np.random.permutation(T2)[:S]),
        "pos1": striped(np.random.permutation(T2)[:P]),
        "pos2": striped(np.random.permutation(T2)[:P]),
    }

def reference(tab_words, tab_scales, tab2_words, tab2_scales, w1, w2_words, w2_scales,
              res, wgs, page0, wl, offs, offs2, offs3, pos1, pos2):
    v = unpack_weight(tab_words, tab_scales, "e4m3")[:, unstriped(offs)]
    v2 = unpack_weight(tab2_words, tab2_scales, "e4m3")[:, unstriped(offs2)]
    w2 = unpack_weight(w2_words, w2_scales, "e2m1")
    phase = mxq(f64(w1), 0, "e4m3").T @ v
    h = np.cos(phase) * (w2.T @ v) + f64(res)
    page = f64(page0).copy()
    page[:, unstriped(offs3)] = np.tile(f64(wgs), (H // 128, 1)) * h
    x = mxq(np.abs(page), 0, "e4m3")
    e = v2.T @ x
    left = f64(wl)[:, None] * e[:, unstriped(pos1)]
    return np.minimum(left, e[:, unstriped(pos2)])

@@ -1,0 +1,304 @@
+import math
+from contextlib import ExitStack
+
+import concourse.mybir as mybir
+
+K, H, T, S, S2, T3, T2, PAIRS = 1024, 1024, 2048, 512, 1024, 2048, 1024, 512
+FLOPS = 2 * (2 * K * H * S + H * S2 * T2)
+
+F32 = mybir.dt.float32
+BF16 = mybir.dt.bfloat16
+I32 = mybir.dt.int32
+U32 = mybir.dt.uint32
+U16 = mybir.dt.uint16
+U8 = mybir.dt.uint8
+FP8X4 = mybir.dt.float8_e4m3fn_x4
+FP4X4 = mybir.dt.float4_e2m1fn_x4
+ALU = mybir.AluOpType
+ACT = mybir.ActivationFunctionType
+
+P = 128
+PACK = 4
+PASS = P * PACK
+BANK = 512
+QUADS = 4
+TWO_PI = 2.0 * math.pi
+
+
+def tile_list_fault_horizon_scores_kernel(
+    tc, tab_words, tab_scales, tab2_words, tab2_scales, w1, w2_words, w2_scales,
+    res, wgs, page0, wl, offs, offs2, offs3, pos1, pos2, out,
+):
+    nc = tc.nc
+    with ExitStack() as ctx:
+        lists = ctx.enter_context(tc.tile_pool(name="lists", bufs=1))
+        held = ctx.enter_context(tc.tile_pool(name="held", bufs=1))
+        work = ctx.enter_context(tc.tile_pool(name="work", bufs=2))
+        psum = ctx.enter_context(tc.psum_pool(name="psum", bufs=8))
+
+        def load_list(src, name):
+            tile = lists.tile(list(src.shape), U16, name=name)
+            nc.sync.dma_start(tile[:], src)
+            return tile
+
+        def load_words(src, a, name):
+            tile = held.tile([P, src.shape[2]], U32, name=name, tag=name, align_bytes=64)
+            nc.sync.dma_start(tile[:].bitcast(I32), src[a].rearrange("p t i -> p (t i)").bitcast(I32))
+            return tile
+
+        def load_w1(a, b):
+            tile = held.tile([P, PACK, PASS], F32, name="w1_raw_%d_%d" % (a, b), tag="w1_raw_%d_%d" % (a, b))
+            rows = w1[a * PASS : (a + 1) * PASS, b * PASS : (b + 1) * PASS]
+            nc.sync.dma_start(tile[:], rows.rearrange("(p j) c -> p j c", j=PACK))
+            return tile
+
+        def load_w2_words():
+            tile = held.tile([P, 2, 2 * H], U8, name="w2_raw")
+            nc.sync.dma_start(tile[:].bitcast(I32), w2_words.rearrange("a p c -> p a c").bitcast(I32))
+            return tile
+
+        def load_planes_side_by_side(src, name, engine):
+            tile = held.tile([P, 2, src.shape[2]], U8, name=name)
+            engine.memset(tile[:].bitcast(I32), 0)
+            for q in range(QUADS):
+                rows = src[:, 4 * q : 4 * q + 4, :].rearrange("a r n -> r a n")
+                nc.sync.dma_start(tile[32 * q : 32 * q + 4, :, :].bitcast(I32), rows.bitcast(I32))
+            return tile
+
+        def load_page(b, t):
+            tile = held.tile([P, T2], F32, name="page_%d_%d" % (b, t))
+            nc.sync.dma_start(tile[:], page0.rearrange("(b p t) n -> b t p n", b=2, t=PACK)[b, t])
+            return tile
+
+        def load_res(b, t0, t1):
+            tile = held.tile([P, t1 - t0, S], F32, name="res_%d_%d" % (b, t0), tag="res_%d_%d" % (b, t0), align_bytes=64)
+            nc.sync.dma_start(tile[:], res.rearrange("(b p t) j -> b p t j", b=2, t=PACK)[b, :, t0:t1, :])
+            return [tile[:, t, :] for t in range(t1 - t0)]
+
+        def load_wgs(t0, t1):
+            tile = held.tile([P, t1 - t0, S], F32, name="wgs_%d" % t0, tag="wgs_%d" % t0, align_bytes=64)
+            rows = wgs.rearrange("(q t) j -> q t j", t=PACK)[:, t0:t1, :]
+            for q in range(QUADS):
+                nc.sync.dma_start(tile[32 * q : 32 * q + 32, :, :], rows)
+            return [tile[:, t, :] for t in range(t1 - t0)]
+
+        tab_w = [load_words(tab_words, 0, "tab_w0")]
+        tab_s = load_planes_side_by_side(tab_scales, "tab_s", nc.vector)
+        idx = load_list(offs, "idx")
+        w1_raw = {(0, 0): load_w1(0, 0)}
+        w2_s_raw = load_planes_side_by_side(w2_scales, "w2_s_raw", nc.gpsimd)
+        w1_raw[(1, 0)] = load_w1(1, 0)
+        tab_w = tab_w + [load_words(tab_words, 1, "tab_w1")]
+        w2_raw = load_w2_words()
+        idx3 = load_list(offs3, "idx3")
+        res_t = load_res(0, 0, 1)
+        wgs_t = load_wgs(0, 2)
+        page = [load_page(0, 0)]
+        w1_raw[(0, 1)] = load_w1(0, 1)
+        page = page + [load_page(0, 1)]
+        res_t = res_t + load_res(0, 1, 4)
+        w1_raw[(1, 1)] = load_w1(1, 1)
+        wgs_t = wgs_t + load_wgs(2, 4)
+        page = page + [load_page(0, 2), load_page(0, 3)]
+        res_t = res_t + load_res(1, 0, 4)
+        page = page + [load_page(1, t) for t in range(PACK)]
+        idx2 = load_list(offs2, "idx2")
+        tab2_s = held.tile([P, T3], U8, name="tab2_s")
+        nc.gpsimd.memset(tab2_s[:].bitcast(I32), 0)
+        for q in range(QUADS):
+            nc.sync.dma_start(tab2_s[32 * q : 32 * q + 8, :].bitcast(I32), tab2_scales[:, 4 * q : 4 * q + 4, :].bitcast(I32))
+        tab2_w = [load_words(tab2_words, a, "tab2_w%d" % a) for a in range(2)]
+        p1 = load_list(pos1, "p1")
+        p2 = load_list(pos2, "p2")
+        wl_col = held.tile([P, S2 // P], F32, name="wl_col")
+        with nc.allow_non_contiguous_dma(reason="one weight a partition"):
+            nc.sync.dma_start(wl_col[:], wl.rearrange("(i p) -> p i", p=P))
+
+        v_w = held.tile([P, 2, S], U32, name="v_w", align_bytes=64)
+        v_s = held.tile([P, 2, S], U8, name="v_s", align_bytes=64)
+
+        def quantise_w1(b):
+            codes = held.tile([P, 2, PASS], U32, name="w1_codes_%d" % b, align_bytes=64)
+            scales = held.tile([P, 2, PASS], U8, name="w1_scales_%d" % b, align_bytes=64)
+            for a in range(2):
+                if b == 0:
+                    grouped = work.tile([P, PASS * PACK], BF16, name="w1_bf", tag="wide", bufs=3, align_bytes=64)
+                else:
+                    grouped = held.tile([P, PASS * PACK], BF16, name="w1_bf_late", tag=("gated_0", "res_0_0")[a], align_bytes=64)
+                dst = grouped[:].rearrange("p (t m j) -> p m t j", t=PACK, j=PACK)
+                src = w1_raw[(a, b)][:].rearrange("p j (m t) -> p m t j", t=PACK)
+                if (a, b) == (1, 0):
+                    nc.vector.tensor_copy(dst, src)
+                else:
+                    nc.scalar.copy(dst, src)
+                nc.vector.quantize_mx(codes[:, a, :].bitcast(FP8X4), scales[:, a, :], grouped[:])
+            return codes, scales
+
+        w2_dealt = held.tile([P, 2, 2, 2 * PASS], U8, name="w2_dealt", tag="tab_w1", align_bytes=64)
+
+        def deal_w2(b):
+            words = w2_dealt[:, b, :, :]
+            scales = held.tile([P, 2, PASS], U8, name="w2_scales_%d" % b, align_bytes=64)
+            nc.vector.tensor_copy(
+                scales[:].rearrange("p a (t m) -> p a t m", t=PACK),
+                w2_s_raw[:, :, b * PASS : (b + 1) * PASS].rearrange("p a (m t) -> p a t m", t=PACK),
+            )
+            nc.vector.tensor_copy(
+                words.bitcast(U16).rearrange("p a (t m) -> p a t m", t=PACK),
+                w2_raw[:].bitcast(U16)[:, :, b * PASS : (b + 1) * PASS].rearrange("p a (m t) -> p a t m", t=PACK),
+            )
+            return words, scales
+
+        for a in range(2):
+            nc.vector.tensor_copy(v_s[:, a, :], tab_s[:, a, :].indirect(idx[:]))
+        nc.vector.tensor_copy(v_w[:, 0, :], tab_w[0][:].indirect(idx[:]))
+        w1_q = {0: quantise_w1(0)}
+        nc.vector.tensor_copy(v_w[:, 1, :], tab_w[1][:].indirect(idx[:]))
+        w2_q = [deal_w2(0), deal_w2(1)]
+
+        spent = {}
+
+        sizes = {}
+
+        def count_turns(i):
+            b, t = divmod(i, PACK)
+            codes, scales = w1_q[b]
+            phase = psum.tile([P, BANK], F32, name="phase", tag="bank")
+            cols = slice(t * P, (t + 1) * P)
+            for a in range(2):
+                nc.tensor.matmul_mx(
+                    phase[:], lhsT=codes[:, a, cols].bitcast(FP8X4), lhsT_scale=scales[:, a, cols],
+                    rhs=v_w[:, a, :].bitcast(FP8X4), rhs_scale=v_s[:, a, :], start=(a == 0), stop=(a == 1),
+                )
+            size = work.tile([P, S], F32, name="size", tag="size")
+            nc.scalar.activation(size[:], phase[:], ACT.Abs)
+            turns = work.tile([P, S], U32, name="turns", tag="turns", bufs=3)
+            nc.scalar.activation(turns[:], size[:], ACT.Copy, scale=1.0 / TWO_PI)
+            spent[i] = turns
+            sizes[i] = size
+
+        def reduce_phase(i):
+            turns, size = spent[i], sizes[i]
+            cosine = work.tile([P, S], F32, name="cosine", tag="cosine", bufs=3)
+            nc.vector.scalar_tensor_tensor(cosine[:], turns[:].bitcast(I32), -TWO_PI, size[:], ALU.mult, ALU.add)
+            nc.scalar.activation(cosine[:], cosine[:], ACT.Abs)
+            nc.scalar.activation(cosine[:], cosine[:], ACT.Sin, bias=math.pi / 2, scale=-1.0)
+            return cosine
+
+        def gate(i, cosine):
+            b, t = divmod(i, PACK)
+            words, scales = w2_q[b]
+            lin = psum.tile([P, BANK], F32, name="lin", tag="bank")
+            for a in range(2):
+                nc.tensor.matmul_mx(
+                    lin[:], lhsT=words[:, a, 2 * t * P : 2 * (t + 1) * P].bitcast(FP4X4),
+                    lhsT_scale=scales[:, a, t * P : (t + 1) * P],
+                    rhs=v_w[:, a, :].bitcast(FP8X4), rhs_scale=v_s[:, a, :], start=(a == 0), stop=(a == 1),
+                )
+            if i < 3:
+                gated = held.tile([P, S], F32, name="gated_early", tag=("gated_0", "gated_0", "res_0_0")[i], align_bytes=64)
+            else:
+                gated = work.tile([P, S], F32, name="gated", tag="gated")
+            nc.vector.tensor_tensor(gated[:], lin[:], cosine[:], ALU.mult)
+            return gated
+
+        def add_res(i, gated):
+            if i + 1 in spent:
+                h = spent[i + 1][:].bitcast(F32)
+            else:
+                h = held.tile([P, S], F32, name="h_%d" % i, tag="h_%d" % i, align_bytes=64)[:]
+            nc.vector.tensor_tensor(h, gated[:], res_t[i], ALU.add)
+            return h
+
+        pairs = [held.tile([P, 2, T2, 2], BF16, name="pairs_%d" % b, tag=("w1_raw_1_1", "pairs_1")[b]) for b in range(2)]
+        x_codes = [held.tile([P, T2], U32, name="x_codes_%d" % b, align_bytes=64) for b in range(2)]
+        x_scales = [held.tile([P, T2], U8, name="x_scales_%d" % b, align_bytes=64) for b in range(2)]
+
+        def magnitudes(i, cols):
+            b, t = divmod(i, PACK)
+            nc.scalar.activation(pairs[b][:, t // 2, cols, t % 2], page[i][:, cols], ACT.Abs)
+
+        def quantise_page(b, cols):
+            grouped = work.tile([P, BANK * PACK], BF16, name="x_bf", tag="wide", bufs=3, align_bytes=64)
+            words = pairs[b][:].rearrange("p u n e -> p u (n e)").bitcast(U32)
+            nc.scalar.copy(
+                grouped[:].bitcast(U32).rearrange("p (n u) -> p n u", u=2),
+                words[:, :, cols].rearrange("p u n -> p n u"),
+            )
+            nc.vector.quantize_mx(x_codes[b][:, cols].bitcast(FP8X4), x_scales[b][:, cols], grouped[:])
+
+        halves = [slice(0, BANK), slice(BANK, 2 * BANK)]
+
+        def place(i, h):
+            b, t = divmod(i, PACK)
+            nc.vector.tensor_tensor(page[i][:].indirect(idx3[:]), h, wgs_t[t], ALU.mult)
+
+        def after_place(i):
+            b, t = divmod(i, PACK)
+            if t < PACK - 1:
+                magnitudes(i, slice(0, T2))
+            else:
+                for cols in halves:
+                    magnitudes(i, cols)
+                    quantise_page(b, cols)
+
+        tiles = 2 * PACK
+        count_turns(0)
+        cosines = {0: reduce_phase(0)}
+        count_turns(1)
+        for i in range(tiles):
+            gated = gate(i, cosines[i])
+            if i + 1 < tiles:
+                cosines[i + 1] = reduce_phase(i + 1)
+            h = add_res(i, gated)
+            if i + 2 < tiles:
+                count_turns(i + 2)
+            place(i, h)
+            if i == 0:
+                w1_q[1] = quantise_w1(1)
+            if i == 2:
+                after_place(0)
+            if i > 1:
+                after_place(i - 1)
+        after_place(tiles - 1)
+
+        v2_s = held.tile([P, S2], U8, name="v2_s", tag="h_7", align_bytes=64)
+        v2_w = held.tile([P, 2, S2], U32, name="v2_w", tag="wgs_2", align_bytes=64)
+        for half in halves:
+            part = idx2[:, half.start // 16 : half.stop // 16]
+            nc.vector.tensor_copy(v2_s[:, half], tab2_s[:].indirect(part))
+            for a in range(2):
+                nc.vector.tensor_copy(v2_w[:, a, half], tab2_w[a][:].indirect(part))
+
+        def scores(i):
+            cols = slice(i * P, (i + 1) * P)
+            e = work.tile([P, T2], F32, name="e", tag="wide", bufs=3, align_bytes=64)
+            for half in halves:
+                bank = psum.tile([P, BANK], F32, name="score", tag="bank")
+                for a in range(2):
+                    nc.tensor.matmul_mx(
+                        bank[:], lhsT=v2_w[:, a, cols].bitcast(FP8X4), lhsT_scale=v2_s[4 * a :, cols],
+                        rhs=x_codes[a][:, half].bitcast(FP8X4), rhs_scale=x_scales[a][:, half],
+                        start=(a == 0), stop=(a == 1),
+                    )
+                nc.scalar.copy(e[:, half], bank[:])
+            return e
+
+        def pick(e):
+            left = work.tile([P, PAIRS], F32, name="left", tag="size")
+            right = work.tile([P, PAIRS], F32, name="right", tag="gated")
+            nc.vector.tensor_copy(left[:], e[:].indirect(p1[:]))
+            nc.vector.tensor_copy(right[:], e[:].indirect(p2[:]))
+            return left, right
+
+        def finish(i, left, right):
+            low = work.tile([P, PAIRS], F32, name="low", tag="cosine", bufs=3)
+            nc.vector.scalar_tensor_tensor(low[:], left[:], wl_col[:, i : i + 1], right[:], ALU.mult, ALU.min)
+            nc.sync.dma_start(out[i * P : (i + 1) * P, :], low[:])
+
+        picked = {}
+        for i in range(S2 // P):
+            picked[i] = pick(scores(i))
+            if i > 0:
+                finish(i - 1, *picked[i - 1])
+        finish(S2 // P - 1, *picked[S2 // P - 1])

@@ -2,6 +2,7 @@ import math
 from contextlib import ExitStack
 
 import concourse.mybir as mybir
+from concourse.masks import make_identity
 
 K, H, T, S, S2, T3, T2, PAIRS = 1024, 1024, 2048, 512, 1024, 2048, 1024, 512
 FLOPS = 2 * (2 * K * H * S + H * S2 * T2)
@@ -34,7 +35,7 @@ def tile_list_fault_horizon_scores_kernel(
         lists = ctx.enter_context(tc.tile_pool(name="lists", bufs=1))
         held = ctx.enter_context(tc.tile_pool(name="held", bufs=1))
         work = ctx.enter_context(tc.tile_pool(name="work", bufs=2))
-        psum = ctx.enter_context(tc.psum_pool(name="psum", bufs=8))
+        psum = ctx.enter_context(tc.psum_pool(name="psum", bufs=1))
 
         def load_list(src, name):
             tile = lists.tile(list(src.shape), U16, name=name)
@@ -57,12 +58,12 @@ def tile_list_fault_horizon_scores_kernel(
             nc.sync.dma_start(tile[:].bitcast(I32), w2_words.rearrange("a p c -> p a c").bitcast(I32))
             return tile
 
-        def load_planes_side_by_side(src, name, engine):
+        def load_planes_side_by_side(src, name, engine, queue):
             tile = held.tile([P, 2, src.shape[2]], U8, name=name)
             engine.memset(tile[:].bitcast(I32), 0)
             for q in range(QUADS):
                 rows = src[:, 4 * q : 4 * q + 4, :].rearrange("a r n -> r a n")
-                nc.sync.dma_start(tile[32 * q : 32 * q + 4, :, :].bitcast(I32), rows.bitcast(I32))
+                queue.dma_start(tile[32 * q : 32 * q + 4, :, :].bitcast(I32), rows.bitcast(I32))
             return tile
 
         def load_page(b, t):
@@ -73,7 +74,7 @@ def tile_list_fault_horizon_scores_kernel(
         def load_res(b, t0, t1):
             tile = held.tile([P, t1 - t0, S], F32, name="res_%d_%d" % (b, t0), tag="res_%d_%d" % (b, t0), align_bytes=64)
             nc.sync.dma_start(tile[:], res.rearrange("(b p t) j -> b p t j", b=2, t=PACK)[b, :, t0:t1, :])
-            return [tile[:, t, :] for t in range(t1 - t0)]
+            return tile
 
         def load_wgs(t0, t1):
             tile = held.tile([P, t1 - t0, S], F32, name="wgs_%d" % t0, tag="wgs_%d" % t0, align_bytes=64)
@@ -82,25 +83,31 @@ def tile_list_fault_horizon_scores_kernel(
                 nc.sync.dma_start(tile[32 * q : 32 * q + 32, :, :], rows)
             return [tile[:, t, :] for t in range(t1 - t0)]
 
-        tab_w = [load_words(tab_words, 0, "tab_w0")]
-        tab_s = load_planes_side_by_side(tab_scales, "tab_s", nc.vector)
+        ident = held.tile([P, P], F32, name="ident")
+        make_identity(nc, ident[:])
+        warm = held.tile([P, 1], F32, name="warm")
+        nc.scalar.activation(warm[:], ident[:, 0:1], ACT.Sin)
+
         idx = load_list(offs, "idx")
-        w1_raw = {(0, 0): load_w1(0, 0)}
-        w2_s_raw = load_planes_side_by_side(w2_scales, "w2_s_raw", nc.gpsimd)
-        w1_raw[(1, 0)] = load_w1(1, 0)
-        tab_w = tab_w + [load_words(tab_words, 1, "tab_w1")]
         w2_raw = load_w2_words()
+        tab_s = load_planes_side_by_side(tab_scales, "tab_s", nc.vector, nc.sync)
+        w1_raw = {(0, 0): load_w1(0, 0)}
+        w2_s_raw = load_planes_side_by_side(w2_scales, "w2_s_raw", nc.gpsimd, nc.sync)
+        w1_raw[(1, 0)] = load_w1(1, 0)
+        tab_w = [load_words(tab_words, a, "tab_w%d" % a) for a in range(2)]
+        for a in range(2):
+            w1_raw[(a, 1)] = load_w1(a, 1)
         idx3 = load_list(offs3, "idx3")
-        res_t = load_res(0, 0, 1)
+        res_g = {(0, 1): load_res(0, 0, 2)[:]}
         wgs_t = load_wgs(0, 2)
         page = [load_page(0, 0)]
-        w1_raw[(0, 1)] = load_w1(0, 1)
         page = page + [load_page(0, 1)]
-        res_t = res_t + load_res(0, 1, 4)
-        w1_raw[(1, 1)] = load_w1(1, 1)
+        res_g[(2, 3)] = load_res(0, 2, 4)[:]
         wgs_t = wgs_t + load_wgs(2, 4)
         page = page + [load_page(0, 2), load_page(0, 3)]
-        res_t = res_t + load_res(1, 0, 4)
+        late = load_res(1, 0, 4)
+        res_g[(4, 5)] = late[:, 0:2, :]
+        res_g[(6, 7)] = late[:, 2:4, :]
         page = page + [load_page(1, t) for t in range(PACK)]
         idx2 = load_list(offs2, "idx2")
         tab2_s = held.tile([P, T3], U8, name="tab2_s")
@@ -117,114 +124,139 @@ def tile_list_fault_horizon_scores_kernel(
         v_w = held.tile([P, 2, S], U32, name="v_w", align_bytes=64)
         v_s = held.tile([P, 2, S], U8, name="v_s", align_bytes=64)
 
-        def quantise_w1(b):
-            codes = held.tile([P, 2, PASS], U32, name="w1_codes_%d" % b, align_bytes=64)
-            scales = held.tile([P, 2, PASS], U8, name="w1_scales_%d" % b, align_bytes=64)
-            for a in range(2):
-                if b == 0:
-                    grouped = work.tile([P, PASS * PACK], BF16, name="w1_bf", tag="wide", bufs=3, align_bytes=64)
-                else:
-                    grouped = held.tile([P, PASS * PACK], BF16, name="w1_bf_late", tag=("gated_0", "res_0_0")[a], align_bytes=64)
-                dst = grouped[:].rearrange("p (t m j) -> p m t j", t=PACK, j=PACK)
-                src = w1_raw[(a, b)][:].rearrange("p j (m t) -> p m t j", t=PACK)
-                if (a, b) == (1, 0):
-                    nc.vector.tensor_copy(dst, src)
-                else:
-                    nc.scalar.copy(dst, src)
-                nc.vector.quantize_mx(codes[:, a, :].bitcast(FP8X4), scales[:, a, :], grouped[:])
-            return codes, scales
-
-        w2_dealt = held.tile([P, 2, 2, 2 * PASS], U8, name="w2_dealt", tag="tab_w1", align_bytes=64)
-
-        def deal_w2(b):
-            words = w2_dealt[:, b, :, :]
-            scales = held.tile([P, 2, PASS], U8, name="w2_scales_%d" % b, align_bytes=64)
-            nc.vector.tensor_copy(
-                scales[:].rearrange("p a (t m) -> p a t m", t=PACK),
-                w2_s_raw[:, :, b * PASS : (b + 1) * PASS].rearrange("p a (m t) -> p a t m", t=PACK),
+        w1_q = [
+            (
+                held.tile([P, 2, PASS], U32, name="w1_codes_%d" % b, align_bytes=64),
+                held.tile([P, 2, PASS], U8, name="w1_scales_%d" % b, align_bytes=64),
             )
+            for b in range(2)
+        ]
+
+        def quantise_w1(a, b):
+            codes, scales = w1_q[b]
+            grouped = work.tile([P, PASS * PACK], BF16, name="w1_bf", tag="wide", bufs=3, align_bytes=64)
+            dst = grouped[:].rearrange("p (t m j) -> p m j t", t=PACK, j=PACK)
+            src = w1_raw[(a, b)][:].rearrange("p j (m t) -> p m j t", t=PACK)
+            nc.scalar.copy(dst, src)
+            nc.vector.quantize_mx(codes[:, a, :].bitcast(FP8X4), scales[:, a, :], grouped[:])
+
+        w2_w = held.tile([P, 2, 2, 2 * PASS], U8, name="w2_w", align_bytes=64)
+        for b in range(2):
             nc.vector.tensor_copy(
-                words.bitcast(U16).rearrange("p a (t m) -> p a t m", t=PACK),
+                w2_w[:, b, :, :].bitcast(U16).rearrange("p a (t m) -> p a t m", t=PACK),
                 w2_raw[:].bitcast(U16)[:, :, b * PASS : (b + 1) * PASS].rearrange("p a (m t) -> p a t m", t=PACK),
             )
-            return words, scales
+
+        def deal_w2_scales():
+            dealt = held.tile([P, 2, 2, PASS], U8, name="w2_s", align_bytes=64)
+            for b in range(2):
+                nc.vector.tensor_copy(
+                    dealt[:, b, :, :].rearrange("p a (t m) -> p a t m", t=PACK),
+                    w2_s_raw[:, :, b * PASS : (b + 1) * PASS].rearrange("p a (m t) -> p a t m", t=PACK),
+                )
+            return dealt
 
         for a in range(2):
             nc.vector.tensor_copy(v_s[:, a, :], tab_s[:, a, :].indirect(idx[:]))
-        nc.vector.tensor_copy(v_w[:, 0, :], tab_w[0][:].indirect(idx[:]))
-        w1_q = {0: quantise_w1(0)}
-        nc.vector.tensor_copy(v_w[:, 1, :], tab_w[1][:].indirect(idx[:]))
-        w2_q = [deal_w2(0), deal_w2(1)]
+        w2_s = deal_w2_scales()
+        quantise_w1(0, 0)
+        quantise_w1(1, 0)
+        for a in range(2):
+            nc.vector.tensor_copy(v_w[:, a, :], tab_w[a][:].indirect(idx[:]))
 
-        spent = {}
+        blocks = [slice(j * P, (j + 1) * P) for j in range(S // P)]
+        parts = {}
+        banks = {}
 
-        sizes = {}
-
-        def count_turns(i):
-            b, t = divmod(i, PACK)
-            codes, scales = w1_q[b]
-            phase = psum.tile([P, BANK], F32, name="phase", tag="bank")
-            cols = slice(t * P, (t + 1) * P)
+        def direct_cosine(i):
+            codes, scales = w1_q[0]
+            phase = psum.tile([P, BANK], F32, name="phase", tag="bank_c", bufs=2)
+            banks[i] = phase
             for a in range(2):
                 nc.tensor.matmul_mx(
-                    phase[:], lhsT=codes[:, a, cols].bitcast(FP8X4), lhsT_scale=scales[:, a, cols],
+                    phase[:], lhsT=codes[:, a, blocks[i]].bitcast(FP8X4), lhsT_scale=scales[:, a, blocks[i]],
                     rhs=v_w[:, a, :].bitcast(FP8X4), rhs_scale=v_s[:, a, :], start=(a == 0), stop=(a == 1),
                 )
-            size = work.tile([P, S], F32, name="size", tag="size")
-            nc.scalar.activation(size[:], phase[:], ACT.Abs)
-            turns = work.tile([P, S], U32, name="turns", tag="turns", bufs=3)
-            nc.scalar.activation(turns[:], size[:], ACT.Copy, scale=1.0 / TWO_PI)
-            spent[i] = turns
-            sizes[i] = size
-
-        def reduce_phase(i):
-            turns, size = spent[i], sizes[i]
-            cosine = work.tile([P, S], F32, name="cosine", tag="cosine", bufs=3)
-            nc.vector.scalar_tensor_tensor(cosine[:], turns[:].bitcast(I32), -TWO_PI, size[:], ALU.mult, ALU.add)
+            turns = work.tile([P, S], U32, name="turns", tag="turns")
+            nc.vector.tensor_scalar(turns[:].bitcast(I32), phase[:], 1.0 / TWO_PI, None, ALU.mult)
+            cosine = work.tile([P, S], F32, name="cosine", tag="cosine", bufs=4)
+            nc.vector.scalar_tensor_tensor(cosine[:], turns[:].bitcast(I32), -TWO_PI, phase[:], ALU.mult, ALU.add)
             nc.scalar.activation(cosine[:], cosine[:], ACT.Abs)
             nc.scalar.activation(cosine[:], cosine[:], ACT.Sin, bias=math.pi / 2, scale=-1.0)
             return cosine
 
-        def gate(i, cosine):
+        def count_turns(i):
             b, t = divmod(i, PACK)
-            words, scales = w2_q[b]
-            lin = psum.tile([P, BANK], F32, name="lin", tag="bank")
+            codes, scales = w1_q[b]
+            phase = psum.tile([P, BANK], F32, name="phase", tag=("bank_c", "bank_a")[b], bufs=(2, 4)[b])
+            banks[i] = phase
+            for a in range(2):
+                for j, cols in enumerate(blocks):
+                    nc.tensor.matmul_mx(
+                        phase[:, cols], lhsT=v_w[:, a, cols].bitcast(FP8X4), lhsT_scale=v_s[:, a, cols],
+                        rhs=codes[:, a, blocks[t]].bitcast(FP8X4), rhs_scale=scales[:, a, blocks[t]],
+                        start=(a == 0 and j == 0), stop=(a == 1 and j == len(blocks) - 1),
+                    )
+            if i == 7:
+                size = held.tile([P, S], F32, name="size_held", tag="w1_raw_1_1")
+            else:
+                size = work.tile([P, S], F32, name="size", tag="size")
+            nc.scalar.activation(size[:], phase[:], ACT.Abs)
+            turns = work.tile([P, S], U32, name="turns", tag="turns")
+            nc.scalar.activation(turns[:], size[:], ACT.Copy, scale=1.0 / TWO_PI)
+            if i == 7:
+                back = held.tile([P, S], F32, name="back_held", tag="pairs_1")
+            else:
+                back = work.tile([P, S], F32, name="back", tag="back")
+            nc.scalar.activation(back[:], turns[:], ACT.Copy, scale=-TWO_PI)
+            parts[i] = (size, back)
+
+        def reduce_phase(i):
+            angle = psum.tile([P, BANK], F32, name="angle", tag="bank_b", bufs=2)
+            for cols in blocks:
+                for n, part in enumerate(parts[i]):
+                    nc.tensor.matmul(
+                        angle[:, cols], lhsT=part[:, cols], rhs=ident[:], is_transpose=True, start=(n == 0), stop=(n == 1)
+                    )
+            cosine = work.tile([P, S], F32, name="cosine", tag="cosine", bufs=4)
+            nc.scalar.activation(cosine[:], angle[:], ACT.Abs)
+            nc.scalar.activation(cosine[:], cosine[:], ACT.Sin, bias=math.pi / 2, scale=-1.0)
+            return cosine
+
+        def gate(i, cosine, gated):
+            b, t = divmod(i, PACK)
+            words, scales = w2_w[:, b, :, :], w2_s[:, b, :, :]
+            lin = banks[i]
             for a in range(2):
                 nc.tensor.matmul_mx(
                     lin[:], lhsT=words[:, a, 2 * t * P : 2 * (t + 1) * P].bitcast(FP4X4),
                     lhsT_scale=scales[:, a, t * P : (t + 1) * P],
                     rhs=v_w[:, a, :].bitcast(FP8X4), rhs_scale=v_s[:, a, :], start=(a == 0), stop=(a == 1),
                 )
-            if i < 3:
-                gated = held.tile([P, S], F32, name="gated_early", tag=("gated_0", "gated_0", "res_0_0")[i], align_bytes=64)
-            else:
-                gated = work.tile([P, S], F32, name="gated", tag="gated")
-            nc.vector.tensor_tensor(gated[:], lin[:], cosine[:], ALU.mult)
-            return gated
+            nc.vector.tensor_tensor(gated, lin[:], cosine[:], ALU.mult)
 
-        def add_res(i, gated):
-            if i + 1 in spent:
-                h = spent[i + 1][:].bitcast(F32)
-            else:
-                h = held.tile([P, S], F32, name="h_%d" % i, tag="h_%d" % i, align_bytes=64)[:]
-            nc.vector.tensor_tensor(h, gated[:], res_t[i], ALU.add)
-            return h
-
-        pairs = [held.tile([P, 2, T2, 2], BF16, name="pairs_%d" % b, tag=("w1_raw_1_1", "pairs_1")[b]) for b in range(2)]
-        x_codes = [held.tile([P, T2], U32, name="x_codes_%d" % b, align_bytes=64) for b in range(2)]
+        pairs = {}
+        x_codes = {}
         x_scales = [held.tile([P, T2], U8, name="x_scales_%d" % b, align_bytes=64) for b in range(2)]
 
         def magnitudes(i, cols):
             b, t = divmod(i, PACK)
+            if b not in pairs:
+                pairs[b] = held.tile([P, 2, T2, 2], BF16, name="pairs", tag=("w1_raw_1_1", "pairs_1")[b])
             nc.scalar.activation(pairs[b][:, t // 2, cols, t % 2], page[i][:, cols], ACT.Abs)
 
         def quantise_page(b, cols):
-            grouped = work.tile([P, BANK * PACK], BF16, name="x_bf", tag="wide", bufs=3, align_bytes=64)
+            if b == 0:
+                grouped = work.tile([P, BANK * PACK], BF16, name="x_bf", tag="wide", bufs=3, align_bytes=64)
+            else:
+                grouped = held.tile([P, BANK * PACK], BF16, name="x_bf_last", tag=("res_0_0", "turn_1")[cols.start // BANK], align_bytes=64)
             words = pairs[b][:].rearrange("p u n e -> p u (n e)").bitcast(U32)
             nc.scalar.copy(
                 grouped[:].bitcast(U32).rearrange("p (n u) -> p n u", u=2),
                 words[:, :, cols].rearrange("p u n -> p n u"),
             )
+            if b not in x_codes:
+                x_codes[b] = held.tile([P, T2], U32, name="x_codes", tag=("turn_0", "x_codes_1")[b], align_bytes=64)
             nc.vector.quantize_mx(x_codes[b][:, cols].bitcast(FP8X4), x_scales[b][:, cols], grouped[:])
 
         halves = [slice(0, BANK), slice(BANK, 2 * BANK)]
@@ -243,41 +275,47 @@ def tile_list_fault_horizon_scores_kernel(
                     quantise_page(b, cols)
 
         tiles = 2 * PACK
-        count_turns(0)
-        cosines = {0: reduce_phase(0)}
-        count_turns(1)
+        groups = [(0, 1), (2, 3), (4, 5), (6, 7)]
+        gated_tags = ["turn_0", "turn_1", "turn_0", "turn_1"]
+        h_tags = ["turn_1", "turn_0", "turn_1", "turn_0"]
+        cosines = {i: direct_cosine(i) for i in range(2)}
+        for a in range(2):
+            quantise_w1(a, 1)
+        for n, group in enumerate(groups):
+            gated = held.tile([P, len(group), S], F32, name="gated", tag=gated_tags[n], align_bytes=64)
+            for m, i in enumerate(group):
+                gate(i, cosines[i], gated[:, m, :])
+            h = held.tile([P, len(group), S], F32, name="h", tag=h_tags[n], align_bytes=64)
+            nc.vector.tensor_tensor(h[:], gated[:], res_g[group], ALU.add)
+            if n + 1 < len(groups):
+                for i in groups[n + 1]:
+                    count_turns(i)
+                    cosines[i] = reduce_phase(i)
+            for m, i in enumerate(group):
+                place(i, h[:, m, :])
         for i in range(tiles):
-            gated = gate(i, cosines[i])
-            if i + 1 < tiles:
-                cosines[i + 1] = reduce_phase(i + 1)
-            h = add_res(i, gated)
-            if i + 2 < tiles:
-                count_turns(i + 2)
-            place(i, h)
-            if i == 0:
-                w1_q[1] = quantise_w1(1)
-            if i == 2:
-                after_place(0)
-            if i > 1:
-                after_place(i - 1)
-        after_place(tiles - 1)
+            after_place(i)
 
-        v2_s = held.tile([P, S2], U8, name="v2_s", tag="h_7", align_bytes=64)
-        v2_w = held.tile([P, 2, S2], U32, name="v2_w", tag="wgs_2", align_bytes=64)
-        for half in halves:
+        v2_s = []
+        v2_w = []
+        for c, half in enumerate(halves):
             part = idx2[:, half.start // 16 : half.stop // 16]
-            nc.vector.tensor_copy(v2_s[:, half], tab2_s[:].indirect(part))
+            v2_s.append(held.tile([P, BANK], U8, name="v2_s", tag=("res_1_0", "res_0_0")[c], align_bytes=64))
+            v2_w.append(held.tile([P, 2, BANK], U32, name="v2_w", tag=("wgs_2", "turn_1")[c], align_bytes=64))
+            nc.vector.tensor_copy(v2_s[c][:], tab2_s[:].indirect(part))
             for a in range(2):
-                nc.vector.tensor_copy(v2_w[:, a, half], tab2_w[a][:].indirect(part))
+                nc.vector.tensor_copy(v2_w[c][:, a, :], tab2_w[a][:].indirect(part))
 
         def scores(i):
-            cols = slice(i * P, (i + 1) * P)
+            c, j = divmod(i, len(blocks))
+            cols = blocks[j]
             e = work.tile([P, T2], F32, name="e", tag="wide", bufs=3, align_bytes=64)
-            for half in halves:
-                bank = psum.tile([P, BANK], F32, name="score", tag="bank")
+            for n, half in enumerate(halves):
+                tag, bufs = (("bank_a", 4), ("bank_b", 2), ("bank_a", 4), ("bank_c", 2))[(2 * i + n) % 4]
+                bank = psum.tile([P, BANK], F32, name="score", tag=tag, bufs=bufs)
                 for a in range(2):
                     nc.tensor.matmul_mx(
-                        bank[:], lhsT=v2_w[:, a, cols].bitcast(FP8X4), lhsT_scale=v2_s[4 * a :, cols],
+                        bank[:], lhsT=v2_w[c][:, a, cols].bitcast(FP8X4), lhsT_scale=v2_s[c][4 * a :, cols],
                         rhs=x_codes[a][:, half].bitcast(FP8X4), rhs_scale=x_scales[a][:, half],
                         start=(a == 0), stop=(a == 1),
                     )
@@ -286,13 +324,13 @@ def tile_list_fault_horizon_scores_kernel(
 
         def pick(e):
             left = work.tile([P, PAIRS], F32, name="left", tag="size")
-            right = work.tile([P, PAIRS], F32, name="right", tag="gated")
+            right = work.tile([P, PAIRS], F32, name="right", tag="back")
             nc.vector.tensor_copy(left[:], e[:].indirect(p1[:]))
             nc.vector.tensor_copy(right[:], e[:].indirect(p2[:]))
             return left, right
 
         def finish(i, left, right):
-            low = work.tile([P, PAIRS], F32, name="low", tag="cosine", bufs=3)
+            low = work.tile([P, PAIRS], F32, name="low", tag="cosine", bufs=4)
             nc.vector.scalar_tensor_tensor(low[:], left[:], wl_col[:, i : i + 1], right[:], ALU.mult, ALU.min)
             nc.sync.dma_start(out[i * P : (i + 1) * P, :], low[:])
 

@@ -124,21 +124,17 @@ def tile_list_fault_horizon_scores_kernel(
         v_w = held.tile([P, 2, S], U32, name="v_w", align_bytes=64)
         v_s = held.tile([P, 2, S], U8, name="v_s", align_bytes=64)
 
-        w1_q = [
-            (
-                held.tile([P, 2, PASS], U32, name="w1_codes_%d" % b, align_bytes=64),
-                held.tile([P, 2, PASS], U8, name="w1_scales_%d" % b, align_bytes=64),
-            )
-            for b in range(2)
-        ]
+        w1_codes = {}
+        w1_scales = [held.tile([P, 2, PASS], U8, name="w1_scales_%d" % b, align_bytes=64) for b in range(2)]
 
         def quantise_w1(a, b):
-            codes, scales = w1_q[b]
+            tag = "tab_w0" if (a, b) == (1, 0) else "w1_codes_%d_%d" % (a, b)
+            w1_codes[(a, b)] = held.tile([P, PASS], U32, name="w1_codes", tag=tag, align_bytes=64)
             grouped = work.tile([P, PASS * PACK], BF16, name="w1_bf", tag="wide", bufs=3, align_bytes=64)
             dst = grouped[:].rearrange("p (t m j) -> p m j t", t=PACK, j=PACK)
             src = w1_raw[(a, b)][:].rearrange("p j (m t) -> p m j t", t=PACK)
             nc.scalar.copy(dst, src)
-            nc.vector.quantize_mx(codes[:, a, :].bitcast(FP8X4), scales[:, a, :], grouped[:])
+            nc.vector.quantize_mx(w1_codes[(a, b)][:].bitcast(FP8X4), w1_scales[b][:, a, :], grouped[:])
 
         w2_w = held.tile([P, 2, 2, 2 * PASS], U8, name="w2_w", align_bytes=64)
         for b in range(2):
@@ -160,21 +156,20 @@ def tile_list_fault_horizon_scores_kernel(
             nc.vector.tensor_copy(v_s[:, a, :], tab_s[:, a, :].indirect(idx[:]))
         w2_s = deal_w2_scales()
         quantise_w1(0, 0)
+        nc.vector.tensor_copy(v_w[:, 0, :], tab_w[0][:].indirect(idx[:]))
         quantise_w1(1, 0)
-        for a in range(2):
-            nc.vector.tensor_copy(v_w[:, a, :], tab_w[a][:].indirect(idx[:]))
+        nc.vector.tensor_copy(v_w[:, 1, :], tab_w[1][:].indirect(idx[:]))
 
         blocks = [slice(j * P, (j + 1) * P) for j in range(S // P)]
         parts = {}
         banks = {}
 
         def direct_cosine(i):
-            codes, scales = w1_q[0]
             phase = psum.tile([P, BANK], F32, name="phase", tag="bank_c", bufs=2)
             banks[i] = phase
             for a in range(2):
                 nc.tensor.matmul_mx(
-                    phase[:], lhsT=codes[:, a, blocks[i]].bitcast(FP8X4), lhsT_scale=scales[:, a, blocks[i]],
+                    phase[:], lhsT=w1_codes[(a, 0)][:, blocks[i]].bitcast(FP8X4), lhsT_scale=w1_scales[0][:, a, blocks[i]],
                     rhs=v_w[:, a, :].bitcast(FP8X4), rhs_scale=v_s[:, a, :], start=(a == 0), stop=(a == 1),
                 )
             turns = work.tile([P, S], U32, name="turns", tag="turns")
@@ -187,14 +182,13 @@ def tile_list_fault_horizon_scores_kernel(
 
         def count_turns(i):
             b, t = divmod(i, PACK)
-            codes, scales = w1_q[b]
             phase = psum.tile([P, BANK], F32, name="phase", tag=("bank_c", "bank_a")[b], bufs=(2, 4)[b])
             banks[i] = phase
             for a in range(2):
                 for j, cols in enumerate(blocks):
                     nc.tensor.matmul_mx(
                         phase[:, cols], lhsT=v_w[:, a, cols].bitcast(FP8X4), lhsT_scale=v_s[:, a, cols],
-                        rhs=codes[:, a, blocks[t]].bitcast(FP8X4), rhs_scale=scales[:, a, blocks[t]],
+                        rhs=w1_codes[(a, b)][:, blocks[t]].bitcast(FP8X4), rhs_scale=w1_scales[b][:, a, blocks[t]],
                         start=(a == 0 and j == 0), stop=(a == 1 and j == len(blocks) - 1),
                     )
             if i == 7:
@@ -322,21 +316,28 @@ def tile_list_fault_horizon_scores_kernel(
                 nc.scalar.copy(e[:, half], bank[:])
             return e
 
-        def pick(e):
+        def pick(e, pieces):
             left = work.tile([P, PAIRS], F32, name="left", tag="size")
             right = work.tile([P, PAIRS], F32, name="right", tag="back")
             nc.vector.tensor_copy(left[:], e[:].indirect(p1[:]))
-            nc.vector.tensor_copy(right[:], e[:].indirect(p2[:]))
+            for cols in pieces:
+                nc.vector.tensor_copy(right[:, cols], e[:].indirect(p2[:, cols.start // 16 : cols.stop // 16]))
             return left, right
 
-        def finish(i, left, right):
+        def finish(i, left, right, pieces):
+            weighted = work.tile([P, PAIRS], F32, name="weighted", tag="turns")
+            nc.scalar.activation(weighted[:], left[:], ACT.Copy, scale=wl_col[:, i : i + 1])
             low = work.tile([P, PAIRS], F32, name="low", tag="cosine", bufs=4)
-            nc.vector.scalar_tensor_tensor(low[:], left[:], wl_col[:, i : i + 1], right[:], ALU.mult, ALU.min)
-            nc.sync.dma_start(out[i * P : (i + 1) * P, :], low[:])
+            for cols in pieces:
+                nc.vector.tensor_tensor(low[:, cols], weighted[:, cols], right[:, cols], ALU.min)
+                nc.sync.dma_start(out[i * P : (i + 1) * P, cols], low[:, cols])
 
-        picked = {}
-        for i in range(S2 // P):
-            picked[i] = pick(scores(i))
-            if i > 0:
-                finish(i - 1, *picked[i - 1])
-        finish(S2 // P - 1, *picked[S2 // P - 1])
+        last = S2 // P - 1
+        whole = [slice(0, PAIRS)]
+        split = [slice(0, PAIRS // 2), slice(PAIRS // 2, PAIRS)]
+        picked = pick(scores(0), whole)
+        for i in range(last):
+            ahead = pick(scores(i + 1), split if i + 1 == last else whole)
+            finish(i, *picked, whole)
+            picked = ahead
+        finish(last, *picked, split)

@@ -318,26 +318,44 @@ def tile_list_fault_horizon_scores_kernel(
 
         def pick(e, pieces):
             left = work.tile([P, PAIRS], F32, name="left", tag="size")
-            right = work.tile([P, PAIRS], F32, name="right", tag="back")
+            right = work.tile([P, PAIRS], F32, name="right", tag="right", bufs=4)
             nc.vector.tensor_copy(left[:], e[:].indirect(p1[:]))
             for cols in pieces:
                 nc.vector.tensor_copy(right[:, cols], e[:].indirect(p2[:, cols.start // 16 : cols.stop // 16]))
             return left, right
 
-        def finish(i, left, right, pieces):
-            weighted = work.tile([P, PAIRS], F32, name="weighted", tag="turns")
+        def weigh(i, left):
+            weighted = work.tile([P, PAIRS], F32, name="weighted", tag="cosine", bufs=4)
             nc.scalar.activation(weighted[:], left[:], ACT.Copy, scale=wl_col[:, i : i + 1])
-            low = work.tile([P, PAIRS], F32, name="low", tag="cosine", bufs=4)
-            for cols in pieces:
-                nc.vector.tensor_tensor(low[:, cols], weighted[:, cols], right[:, cols], ALU.min)
-                nc.sync.dma_start(out[i * P : (i + 1) * P, cols], low[:, cols])
+            return weighted
+
+        def finish(i, weighted, over):
+            low = work.tile([P, PAIRS], F32, name="low", tag="back")
+            nc.gpsimd.tensor_tensor(low[:], weighted[:], over[:], ALU.subtract)
+            nc.sync.dma_start(out[i * P : (i + 1) * P, :], low[:])
 
         last = S2 // P - 1
         whole = [slice(0, PAIRS)]
         split = [slice(0, PAIRS // 2), slice(PAIRS // 2, PAIRS)]
-        picked = pick(scores(0), whole)
-        for i in range(last):
-            ahead = pick(scores(i + 1), split if i + 1 == last else whole)
-            finish(i, *picked, whole)
-            picked = ahead
-        finish(last, *picked, split)
+        def finish_direct(i, weighted, right, pieces):
+            low = work.tile([P, PAIRS], F32, name="low", tag="turns")
+            for cols in pieces:
+                nc.vector.tensor_tensor(low[:, cols], weighted[:, cols], right[:, cols], ALU.min)
+                nc.sync.dma_start(out[i * P : (i + 1) * P, cols], low[:, cols])
+
+        handed = last - 1
+        e_tiles = {0: scores(0)}
+        parts_of = {}
+        for i in range(last + 1):
+            if i < last:
+                e_tiles[i + 1] = scores(i + 1)
+            left, right = pick(e_tiles[i], split if i == last else whole)
+            parts_of[i] = (weigh(i, left), right)
+            if i < handed:
+                nc.gpsimd.tensor_tensor(right[:], parts_of[i][0][:], right[:], ALU.subtract)
+            if 0 < i <= handed:
+                over = parts_of[i - 1][1]
+                nc.scalar.activation(over[:], over[:], ACT.Relu)
+                finish(i - 1, *parts_of[i - 1])
+        finish_direct(last - 1, *parts_of[last - 1], whole)
+        finish_direct(last, *parts_of[last], split)

import math
from contextlib import ExitStack

import concourse.mybir as mybir
from concourse.masks import make_identity

K, H, T, S, S2, T3, T2, PAIRS = 1024, 1024, 2048, 512, 1024, 2048, 1024, 512
FLOPS = 2 * (2 * K * H * S + H * S2 * T2)

F32 = mybir.dt.float32
BF16 = mybir.dt.bfloat16
I32 = mybir.dt.int32
U32 = mybir.dt.uint32
U16 = mybir.dt.uint16
U8 = mybir.dt.uint8
FP8X4 = mybir.dt.float8_e4m3fn_x4
FP4X4 = mybir.dt.float4_e2m1fn_x4
ALU = mybir.AluOpType
ACT = mybir.ActivationFunctionType

P = 128
PACK = 4
PASS = P * PACK
BANK = 512
QUADS = 4
TWO_PI = 2.0 * math.pi


def tile_list_fault_horizon_scores_kernel(
    tc, tab_words, tab_scales, tab2_words, tab2_scales, w1, w2_words, w2_scales,
    res, wgs, page0, wl, offs, offs2, offs3, pos1, pos2, out,
):
    nc = tc.nc
    with ExitStack() as ctx:
        lists = ctx.enter_context(tc.tile_pool(name="lists", bufs=1))
        held = ctx.enter_context(tc.tile_pool(name="held", bufs=1))
        work = ctx.enter_context(tc.tile_pool(name="work", bufs=2))
        psum = ctx.enter_context(tc.psum_pool(name="psum", bufs=1))

        def load_list(src, name):
            tile = lists.tile(list(src.shape), U16, name=name)
            nc.sync.dma_start(tile[:], src)
            return tile

        def load_words(src, a, name):
            tile = held.tile([P, src.shape[2]], U32, name=name, tag=name, align_bytes=64)
            nc.sync.dma_start(tile[:].bitcast(I32), src[a].rearrange("p t i -> p (t i)").bitcast(I32))
            return tile

        def load_w1(a, b):
            tile = held.tile([P, PACK, PASS], F32, name="w1_raw_%d_%d" % (a, b), tag="w1_raw_%d_%d" % (a, b))
            rows = w1[a * PASS : (a + 1) * PASS, b * PASS : (b + 1) * PASS]
            nc.sync.dma_start(tile[:], rows.rearrange("(p j) c -> p j c", j=PACK))
            return tile

        def load_w2_words():
            tile = held.tile([P, 2, 2 * H], U8, name="w2_raw")
            nc.sync.dma_start(tile[:].bitcast(I32), w2_words.rearrange("a p c -> p a c").bitcast(I32))
            return tile

        def load_planes_side_by_side(src, name, engine, queue):
            tile = held.tile([P, 2, src.shape[2]], U8, name=name)
            engine.memset(tile[:].bitcast(I32), 0)
            for q in range(QUADS):
                rows = src[:, 4 * q : 4 * q + 4, :].rearrange("a r n -> r a n")
                queue.dma_start(tile[32 * q : 32 * q + 4, :, :].bitcast(I32), rows.bitcast(I32))
            return tile

        def load_page(b, t):
            tile = held.tile([P, T2], F32, name="page_%d_%d" % (b, t))
            nc.sync.dma_start(tile[:], page0.rearrange("(b p t) n -> b t p n", b=2, t=PACK)[b, t])
            return tile

        def load_res(b, t0, t1):
            tile = held.tile([P, t1 - t0, S], F32, name="res_%d_%d" % (b, t0), tag="res_%d_%d" % (b, t0), align_bytes=64)
            nc.sync.dma_start(tile[:], res.rearrange("(b p t) j -> b p t j", b=2, t=PACK)[b, :, t0:t1, :])
            return tile

        def load_wgs(t0, t1):
            tile = held.tile([P, t1 - t0, S], F32, name="wgs_%d" % t0, tag="wgs_%d" % t0, align_bytes=64)
            rows = wgs.rearrange("(q t) j -> q t j", t=PACK)[:, t0:t1, :]
            for q in range(QUADS):
                nc.sync.dma_start(tile[32 * q : 32 * q + 32, :, :], rows)
            return [tile[:, t, :] for t in range(t1 - t0)]

        ident = held.tile([P, P], F32, name="ident")
        make_identity(nc, ident[:])
        warm = held.tile([P, 1], F32, name="warm")
        nc.scalar.activation(warm[:], ident[:, 0:1], ACT.Sin)

        idx = load_list(offs, "idx")
        w2_raw = load_w2_words()
        tab_s = load_planes_side_by_side(tab_scales, "tab_s", nc.vector, nc.sync)
        w1_raw = {(0, 0): load_w1(0, 0)}
        w2_s_raw = load_planes_side_by_side(w2_scales, "w2_s_raw", nc.gpsimd, nc.sync)
        w1_raw[(1, 0)] = load_w1(1, 0)
        tab_w = [load_words(tab_words, a, "tab_w%d" % a) for a in range(2)]
        for a in range(2):
            w1_raw[(a, 1)] = load_w1(a, 1)
        idx3 = load_list(offs3, "idx3")
        res_g = {(0, 1): load_res(0, 0, 2)[:]}
        wgs_t = load_wgs(0, 2)
        page = [load_page(0, 0)]
        page = page + [load_page(0, 1)]
        res_g[(2, 3)] = load_res(0, 2, 4)[:]
        wgs_t = wgs_t + load_wgs(2, 4)
        page = page + [load_page(0, 2), load_page(0, 3)]
        late = load_res(1, 0, 4)
        res_g[(4, 5)] = late[:, 0:2, :]
        res_g[(6, 7)] = late[:, 2:4, :]
        page = page + [load_page(1, t) for t in range(PACK)]
        idx2 = load_list(offs2, "idx2")
        tab2_s = held.tile([P, T3], U8, name="tab2_s")
        nc.gpsimd.memset(tab2_s[:].bitcast(I32), 0)
        for q in range(QUADS):
            nc.sync.dma_start(tab2_s[32 * q : 32 * q + 8, :].bitcast(I32), tab2_scales[:, 4 * q : 4 * q + 4, :].bitcast(I32))
        tab2_w = [load_words(tab2_words, a, "tab2_w%d" % a) for a in range(2)]
        p1 = load_list(pos1, "p1")
        p2 = load_list(pos2, "p2")
        wl_col = held.tile([P, S2 // P], F32, name="wl_col")
        with nc.allow_non_contiguous_dma(reason="one weight a partition"):
            nc.sync.dma_start(wl_col[:], wl.rearrange("(i p) -> p i", p=P))

        v_w = held.tile([P, 2, S], U32, name="v_w", align_bytes=64)
        v_s = held.tile([P, 2, S], U8, name="v_s", align_bytes=64)

        w1_codes = {}
        w1_scales = [held.tile([P, 2, PASS], U8, name="w1_scales_%d" % b, align_bytes=64) for b in range(2)]

        def quantise_w1(a, b):
            tag = "tab_w0" if (a, b) == (1, 0) else "w1_codes_%d_%d" % (a, b)
            w1_codes[(a, b)] = held.tile([P, PASS], U32, name="w1_codes", tag=tag, align_bytes=64)
            grouped = work.tile([P, PASS * PACK], BF16, name="w1_bf", tag="wide", bufs=3, align_bytes=64)
            dst = grouped[:].rearrange("p (t m j) -> p m j t", t=PACK, j=PACK)
            src = w1_raw[(a, b)][:].rearrange("p j (m t) -> p m j t", t=PACK)
            nc.scalar.copy(dst, src)
            nc.vector.quantize_mx(w1_codes[(a, b)][:].bitcast(FP8X4), w1_scales[b][:, a, :], grouped[:])

        w2_w = held.tile([P, 2, 2, 2 * PASS], U8, name="w2_w", align_bytes=64)
        for b in range(2):
            nc.vector.tensor_copy(
                w2_w[:, b, :, :].bitcast(U16).rearrange("p a (t m) -> p a t m", t=PACK),
                w2_raw[:].bitcast(U16)[:, :, b * PASS : (b + 1) * PASS].rearrange("p a (m t) -> p a t m", t=PACK),
            )

        def deal_w2_scales():
            dealt = held.tile([P, 2, 2, PASS], U8, name="w2_s", align_bytes=64)
            for b in range(2):
                nc.vector.tensor_copy(
                    dealt[:, b, :, :].rearrange("p a (t m) -> p a t m", t=PACK),
                    w2_s_raw[:, :, b * PASS : (b + 1) * PASS].rearrange("p a (m t) -> p a t m", t=PACK),
                )
            return dealt

        for a in range(2):
            nc.vector.tensor_copy(v_s[:, a, :], tab_s[:, a, :].indirect(idx[:]))
        w2_s = deal_w2_scales()
        quantise_w1(0, 0)
        nc.vector.tensor_copy(v_w[:, 0, :], tab_w[0][:].indirect(idx[:]))
        quantise_w1(1, 0)
        nc.vector.tensor_copy(v_w[:, 1, :], tab_w[1][:].indirect(idx[:]))

        blocks = [slice(j * P, (j + 1) * P) for j in range(S // P)]
        parts = {}
        banks = {}

        def direct_cosine(i):
            phase = psum.tile([P, BANK], F32, name="phase", tag="bank_c", bufs=2)
            banks[i] = phase
            for a in range(2):
                nc.tensor.matmul_mx(
                    phase[:], lhsT=w1_codes[(a, 0)][:, blocks[i]].bitcast(FP8X4), lhsT_scale=w1_scales[0][:, a, blocks[i]],
                    rhs=v_w[:, a, :].bitcast(FP8X4), rhs_scale=v_s[:, a, :], start=(a == 0), stop=(a == 1),
                )
            turns = work.tile([P, S], U32, name="turns", tag="turns")
            nc.vector.tensor_scalar(turns[:].bitcast(I32), phase[:], 1.0 / TWO_PI, None, ALU.mult)
            cosine = work.tile([P, S], F32, name="cosine", tag="cosine", bufs=4)
            nc.vector.scalar_tensor_tensor(cosine[:], turns[:].bitcast(I32), -TWO_PI, phase[:], ALU.mult, ALU.add)
            nc.scalar.activation(cosine[:], cosine[:], ACT.Abs)
            nc.scalar.activation(cosine[:], cosine[:], ACT.Sin, bias=math.pi / 2, scale=-1.0)
            return cosine

        def count_turns(i):
            b, t = divmod(i, PACK)
            phase = psum.tile([P, BANK], F32, name="phase", tag=("bank_c", "bank_a")[b], bufs=(2, 4)[b])
            banks[i] = phase
            for a in range(2):
                for j, cols in enumerate(blocks):
                    nc.tensor.matmul_mx(
                        phase[:, cols], lhsT=v_w[:, a, cols].bitcast(FP8X4), lhsT_scale=v_s[:, a, cols],
                        rhs=w1_codes[(a, b)][:, blocks[t]].bitcast(FP8X4), rhs_scale=w1_scales[b][:, a, blocks[t]],
                        start=(a == 0 and j == 0), stop=(a == 1 and j == len(blocks) - 1),
                    )
            if i == 7:
                size = held.tile([P, S], F32, name="size_held", tag="w1_raw_1_1")
            else:
                size = work.tile([P, S], F32, name="size", tag="size")
            nc.scalar.activation(size[:], phase[:], ACT.Abs)
            turns = work.tile([P, S], U32, name="turns", tag="turns")
            nc.scalar.activation(turns[:], size[:], ACT.Copy, scale=1.0 / TWO_PI)
            if i == 7:
                back = held.tile([P, S], F32, name="back_held", tag="pairs_1")
            else:
                back = work.tile([P, S], F32, name="back", tag="back")
            nc.scalar.activation(back[:], turns[:], ACT.Copy, scale=-TWO_PI)
            parts[i] = (size, back)

        def reduce_phase(i):
            angle = psum.tile([P, BANK], F32, name="angle", tag="bank_b", bufs=2)
            for cols in blocks:
                for n, part in enumerate(parts[i]):
                    nc.tensor.matmul(
                        angle[:, cols], lhsT=part[:, cols], rhs=ident[:], is_transpose=True, start=(n == 0), stop=(n == 1)
                    )
            cosine = work.tile([P, S], F32, name="cosine", tag="cosine", bufs=4)
            nc.scalar.activation(cosine[:], angle[:], ACT.Abs)
            nc.scalar.activation(cosine[:], cosine[:], ACT.Sin, bias=math.pi / 2, scale=-1.0)
            return cosine

        def gate(i, cosine, gated):
            b, t = divmod(i, PACK)
            words, scales = w2_w[:, b, :, :], w2_s[:, b, :, :]
            lin = banks[i]
            for a in range(2):
                nc.tensor.matmul_mx(
                    lin[:], lhsT=words[:, a, 2 * t * P : 2 * (t + 1) * P].bitcast(FP4X4),
                    lhsT_scale=scales[:, a, t * P : (t + 1) * P],
                    rhs=v_w[:, a, :].bitcast(FP8X4), rhs_scale=v_s[:, a, :], start=(a == 0), stop=(a == 1),
                )
            nc.vector.tensor_tensor(gated, lin[:], cosine[:], ALU.mult)

        pairs = {}
        x_codes = {}
        x_scales = [held.tile([P, T2], U8, name="x_scales_%d" % b, align_bytes=64) for b in range(2)]

        def magnitudes(i, cols):
            b, t = divmod(i, PACK)
            if b not in pairs:
                pairs[b] = held.tile([P, 2, T2, 2], BF16, name="pairs", tag=("w1_raw_1_1", "pairs_1")[b])
            nc.scalar.activation(pairs[b][:, t // 2, cols, t % 2], page[i][:, cols], ACT.Abs)

        def quantise_page(b, cols):
            if b == 0:
                grouped = work.tile([P, BANK * PACK], BF16, name="x_bf", tag="wide", bufs=3, align_bytes=64)
            else:
                grouped = held.tile([P, BANK * PACK], BF16, name="x_bf_last", tag=("res_0_0", "turn_1")[cols.start // BANK], align_bytes=64)
            words = pairs[b][:].rearrange("p u n e -> p u (n e)").bitcast(U32)
            nc.scalar.copy(
                grouped[:].bitcast(U32).rearrange("p (n u) -> p n u", u=2),
                words[:, :, cols].rearrange("p u n -> p n u"),
            )
            if b not in x_codes:
                x_codes[b] = held.tile([P, T2], U32, name="x_codes", tag=("turn_0", "x_codes_1")[b], align_bytes=64)
            nc.vector.quantize_mx(x_codes[b][:, cols].bitcast(FP8X4), x_scales[b][:, cols], grouped[:])

        halves = [slice(0, BANK), slice(BANK, 2 * BANK)]

        def place(i, h):
            b, t = divmod(i, PACK)
            nc.vector.tensor_tensor(page[i][:].indirect(idx3[:]), h, wgs_t[t], ALU.mult)

        def after_place(i):
            b, t = divmod(i, PACK)
            if t < PACK - 1:
                magnitudes(i, slice(0, T2))
            else:
                for cols in halves:
                    magnitudes(i, cols)
                    quantise_page(b, cols)

        tiles = 2 * PACK
        groups = [(0, 1), (2, 3), (4, 5), (6, 7)]
        gated_tags = ["turn_0", "turn_1", "turn_0", "turn_1"]
        h_tags = ["turn_1", "turn_0", "turn_1", "turn_0"]
        cosines = {i: direct_cosine(i) for i in range(2)}
        for a in range(2):
            quantise_w1(a, 1)
        for n, group in enumerate(groups):
            gated = held.tile([P, len(group), S], F32, name="gated", tag=gated_tags[n], align_bytes=64)
            for m, i in enumerate(group):
                gate(i, cosines[i], gated[:, m, :])
            h = held.tile([P, len(group), S], F32, name="h", tag=h_tags[n], align_bytes=64)
            nc.vector.tensor_tensor(h[:], gated[:], res_g[group], ALU.add)
            if n + 1 < len(groups):
                for i in groups[n + 1]:
                    count_turns(i)
                    cosines[i] = reduce_phase(i)
            for m, i in enumerate(group):
                place(i, h[:, m, :])
        for i in range(tiles):
            after_place(i)

        v2_s = []
        v2_w = []
        for c, half in enumerate(halves):
            part = idx2[:, half.start // 16 : half.stop // 16]
            v2_s.append(held.tile([P, BANK], U8, name="v2_s", tag=("res_1_0", "res_0_0")[c], align_bytes=64))
            v2_w.append(held.tile([P, 2, BANK], U32, name="v2_w", tag=("wgs_2", "turn_1")[c], align_bytes=64))
            nc.vector.tensor_copy(v2_s[c][:], tab2_s[:].indirect(part))
            for a in range(2):
                nc.vector.tensor_copy(v2_w[c][:, a, :], tab2_w[a][:].indirect(part))

        def scores(i):
            c, j = divmod(i, len(blocks))
            cols = blocks[j]
            e = work.tile([P, T2], F32, name="e", tag="wide", bufs=3, align_bytes=64)
            for n, half in enumerate(halves):
                tag, bufs = (("bank_a", 4), ("bank_b", 2), ("bank_a", 4), ("bank_c", 2))[(2 * i + n) % 4]
                bank = psum.tile([P, BANK], F32, name="score", tag=tag, bufs=bufs)
                for a in range(2):
                    nc.tensor.matmul_mx(
                        bank[:], lhsT=v2_w[c][:, a, cols].bitcast(FP8X4), lhsT_scale=v2_s[c][4 * a :, cols],
                        rhs=x_codes[a][:, half].bitcast(FP8X4), rhs_scale=x_scales[a][:, half],
                        start=(a == 0), stop=(a == 1),
                    )
                nc.scalar.copy(e[:, half], bank[:])
            return e

        def pick(e, pieces):
            left = work.tile([P, PAIRS], F32, name="left", tag="size")
            right = work.tile([P, PAIRS], F32, name="right", tag="right", bufs=4)
            nc.vector.tensor_copy(left[:], e[:].indirect(p1[:]))
            for cols in pieces:
                nc.vector.tensor_copy(right[:, cols], e[:].indirect(p2[:, cols.start // 16 : cols.stop // 16]))
            return left, right

        def weigh(i, left):
            weighted = work.tile([P, PAIRS], F32, name="weighted", tag="cosine", bufs=4)
            nc.scalar.activation(weighted[:], left[:], ACT.Copy, scale=wl_col[:, i : i + 1])
            return weighted

        def finish(i, weighted, over):
            low = work.tile([P, PAIRS], F32, name="low", tag="back")
            nc.gpsimd.tensor_tensor(low[:], weighted[:], over[:], ALU.subtract)
            nc.sync.dma_start(out[i * P : (i + 1) * P, :], low[:])

        last = S2 // P - 1
        whole = [slice(0, PAIRS)]
        split = [slice(0, PAIRS // 2), slice(PAIRS // 2, PAIRS)]
        def finish_direct(i, weighted, right, pieces):
            low = work.tile([P, PAIRS], F32, name="low", tag="turns")
            for cols in pieces:
                nc.vector.tensor_tensor(low[:, cols], weighted[:, cols], right[:, cols], ALU.min)
                nc.sync.dma_start(out[i * P : (i + 1) * P, cols], low[:, cols])

        handed = last - 1
        e_tiles = {0: scores(0)}
        parts_of = {}
        for i in range(last + 1):
            if i < last:
                e_tiles[i + 1] = scores(i + 1)
            left, right = pick(e_tiles[i], split if i == last else whole)
            parts_of[i] = (weigh(i, left), right)
            if i < handed:
                nc.gpsimd.tensor_tensor(right[:], parts_of[i][0][:], right[:], ALU.subtract)
            if 0 < i <= handed:
                over = parts_of[i - 1][1]
                nc.scalar.activation(over[:], over[:], ACT.Relu)
                finish(i - 1, *parts_of[i - 1])
        finish_direct(last - 1, *parts_of[last - 1], whole)
        finish_direct(last, *parts_of[last], split)
